import numpy as np, ml_dtypes
CORES = [2,34,66,98,130,162,194,226,258,290,322,354,386,418,450,482]
N = 16
import mx_ref
NC, GR, GC, KT = 256, 4, 4, 1
TS = GC * KT
CH = GR * NC // GC
BF = ml_dtypes.bfloat16
def setup_inputs(rng):
    def f(*shape):
        return mx_ref.flush((rng.standard_normal(shape, dtype=np.float32) * np.exp2(rng.integers(-2, 3, shape[:-1] + (1,)))).astype(BF))
    return {"w": f(N, 128, KT * 512), "x": f(N, 128, KT * 4 * NC)}
def setup_inputs_blocks(rng):
    d = setup_inputs(rng)
    for k in ("w", "x"): d[k] = mx_ref.spread(d[k], rng, 1)
    return d
def setup_inputs_wide(rng):
    d = setup_inputs(rng)
    for k in ("w", "x"): d[k] = mx_ref.flush((d[k].astype(np.float32) * np.exp2(rng.integers(-8, 9, (N, 1, 1))).astype(np.float32)).astype(BF))
    return d
def setup_inputs_zeros(rng):
    d = setup_inputs(rng); v = d["x"].reshape(N, 128, -1, 4).copy()
    v[np.broadcast_to((rng.random((N, 1, v.shape[2], 1)) < 0.33), v.shape)] = 0
    d["x"] = v.reshape(d["x"].shape)
    return d
def reference(w, x):
    QX = [[mx_ref.quantize(x[r][:, 4 * NC * t:4 * NC * t + 4 * NC]) for t in range(KT)] for r in range(N)]
    y = np.zeros((N, 128, CH), np.float32)
    for i in range(GR):
        for s in range(TS):
            k, t = s // KT, s % KT
            qw = mx_ref.quantize(w[i * GC + k][:, 512 * t:512 * t + 512])
            p = np.concatenate([mx_ref.matmul(qw, QX[g * GC + k][t]) for g in range(GR)], axis=1)
            Y = p if s == 0 else Y + p
        for c in range(GC):
            y[i * GC + c] = Y[:, CH * c:CH * c + CH]
    return {"y": y}

@@ -1,0 +1,203 @@
+from concourse.bass import DstId, RemoteDMATransfer
+from concourse.mybir import dt
+
+GR, GC = 4, 4
+XC, WC = 256, 128
+SIM_CORES = 512
+
+ORDER = ["Wh", "a", "Xh", "b", "f"]
+XH = "c"
+W_HELPERS = 1
+H_ENGINES = 8
+W_ON, X_ON = "low", "high"
+HELPER_DIE = "far"
+
+SCRATCH = {
+    "wb": ("sbuf", [128, 4 * WC], "bfloat16"),
+    "xb": ("sbuf", [128, 4 * XC], "bfloat16"),
+    "xo": ("sbuf", [128, XC], "float8_e4m3fn_x4"),
+    "xos": ("sbuf", [128, XC], "uint8"),
+    "xq": ("sbuf", [128, GC * XC], "float8_e4m3fn_x4"),
+    "xs": ("sbuf", [128, GC * XC], "uint8"),
+    "wq": ("sbuf", [128, GC * WC], "float8_e4m3fn_x4"),
+    "ws": ("sbuf", [128, GC * WC], "uint8"),
+    "acc": ("psum", [128, 512], "float32"),
+    "yb": ("sbuf", [128, XC], "float32"),
+}
+PLANE = {"xo": "xos", "xq": "xs", "wq": "ws"}
+SEMAPHORES = (["ldw", "ldx", "qw", "qx", "mm", "cp", "st", "sent", "sxo"]
+              + ["sx%d" % s for s in range(GC)] + ["sw%d" % s for s in range(GC)])
+
+_CACHE = {}
+
+
+def _bits(m):
+    return bin(m).count("1")
+
+
+def _lowest(m, n):
+    out = 0
+    for e in range(m.bit_length()):
+        if m >> e & 1 and _bits(out) < n:
+            out |= 1 << e
+    return out
+
+
+def _plan(T, topo):
+    if "p" in _CACHE:
+        return _CACHE["p"]
+    R = [[T.cores[i * GC + k] for k in range(GC)] for i in range(GR)]
+    steps, inc, order = {}, {}, {}
+
+    def add(src, waits, buf, lo, hi, dsts, sem, mask=None, engines=None):
+        m = mask
+        if m is None:
+            m = topo.mask(src, dsts[0][0])
+            for d in dsts:
+                m &= topo.mask(src, d[0])
+        if engines:
+            m = _lowest(m, engines)
+        steps.setdefault(src, []).append({"wait": waits, "buf": buf, "lo": lo, "hi": hi, "dsts": dsts, "sem": sem, "mask": m})
+        for d in dsts:
+            inc[(d[0], sem)] = inc.get((d[0], sem), 0) + 2 * _bits(m)
+
+    def hosts_of(c):
+        others = [h for h in range(GR) if h != c]
+        diag = [h for h in others if not topo.may_write(R[c][0], R[h][0])][0]
+        mate = [h for h in others if h != diag and topo.rack(topo.host(R[h][0])) == topo.rack(topo.host(R[c][0]))][0]
+        cabl = [h for h in others if h not in (diag, mate)][0]
+        return diag, mate, cabl
+
+    for i in range(GR):
+        diag, mate, cabl = hosts_of(i)
+        for j in range(GC):
+            me = R[i][j]
+            chipmates = [q for q in range(SIM_CORES) if q != me and topo.host(q) == topo.host(me) and topo.chip(q) == topo.chip(me)]
+            helpers = [q for q in chipmates if (topo.die(q) != topo.die(me)) == (HELPER_DIE == "far")]
+            off = topo.mask(me, R[i][(j + 1) % GC])
+
+            def on_chip(q, which):
+                m = topo.mask(me, q)
+                return {"low": m & off, "high": m & ~off, "all": m}[which]
+
+            sw, sx = "sw%d" % j, "sx%d" % j
+            wdst = [(R[i][(j + t) % GC], "wq", j * WC) for t in range(1, GC)]
+            first, second = (cabl, mate) if j // 2 == i // 2 else (mate, cabl)
+            place = {"a": (R[first][i], "xq", j * XC), "b": (R[second][i], "xq", j * XC), "c": (R[i][i], "xq", j * XC)}
+            seen = set()
+
+            def need(name):
+                if name in seen:
+                    return []
+                seen.add(name)
+                return [name]
+
+            for tok in ORDER:
+                if tok == "Wh":
+                    hs = helpers[:W_HELPERS]
+                    add(me, need("qw"), "wq", j * WC, (j + 1) * WC, [(h, "wq", j * WC) for h in hs], sw, on_chip(hs[0], W_ON))
+                    for n, h in enumerate(hs):
+                        add(h, [sw], "wq", j * WC, (j + 1) * WC, wdst[n::W_HELPERS], sw, None, H_ENGINES)
+                elif tok == "W":
+                    add(me, need("qw"), "wq", j * WC, (j + 1) * WC, wdst, sw)
+                elif tok in place:
+                    if place[tok][0] != me:
+                        add(me, need("qx"), "xo", 0, XC, [place[tok]], sx)
+                elif tok == "Xh":
+                    outs = [place[t] for t in XH if place[t][0] != me]
+                    if outs:
+                        h = helpers[W_HELPERS]
+                        add(me, need("qx"), "xo", 0, XC, [(h, "xo", 0)], "sxo", on_chip(h, X_ON))
+                        add(h, ["sxo"], "xo", 0, XC, outs, sx, None, H_ENGINES)
+                elif tok == "f" and j in (mate, cabl):
+                    dj, mj, cj = hosts_of(j)
+                    p = j // 2 if i == cj else 1 - j // 2
+                    add(me, ["sx%d" % (2 * p), "sx%d" % (2 * p + 1)], "xq", 2 * p * XC, (2 * p + 2) * XC,
+                        [(R[dj][j], "xq", 2 * p * XC)], "sx%d" % (2 * p))
+                    order[me] = [2 * p, 2 * p + 1, 2 - 2 * p, 3 - 2 * p]
+            if j == i:
+                order[me] = [j] + [s for s in range(GC) if s != j]
+            elif j == diag:
+                order[me] = [0, 1, 2, 3]
+    _CACHE["p"] = (steps, inc, order)
+    return _CACHE["p"]
+
+
+def _sends(g, T, topo, core, steps, inc):
+    sent = 0
+    for st in steps:
+        for name in st["wait"]:
+            g.wait_ge(T.sem[name], inc.get((core, name), 1))
+        lo, hi, m = st["lo"], st["hi"], st["mask"]
+        for plane in (False, True):
+            if plane:
+                src = T[PLANE[st["buf"]]][:, lo:hi]
+                outs = [T[PLANE[b]][:, a:a + hi - lo] for (_, b, a) in st["dsts"]]
+            else:
+                src = T[st["buf"]][:, lo:hi].bitcast(dt.uint8)
+                outs = [T[b][:, a:a + hi - lo].bitcast(dt.uint8) for (_, b, a) in st["dsts"]]
+            ids = [topo.addr(d[0], core) for d in st["dsts"]]
+            if len(outs) == 1:
+                g.remote_dma(out_ap=outs[0], in_ap=src, remote_sem=T.sem[st["sem"]], local_sem=T.sem.sent,
+                             pid=ids[0][1], routing_id=ids[0][0], dma_engine_mask=m)
+            else:
+                g.remote_dma_fused([RemoteDMATransfer(dst_ids=[DstId(rid=a, pnc=b) for (a, b) in ids], dma_engine_mask=m,
+                                                      remote_sem=T.sem[st["sem"]], srcs=[src], dsts=outs)],
+                                   local_sem=T.sem.sent)
+            sent += _bits(m)
+    if sent:
+        g.wait_ge(T.sem.sent, sent)
+
+
+def rank_program(g, core, T, topo):
+    steps, inc, order = _plan(T, topo)
+    rank = T.rank_of(core)
+    if rank is None:
+        if core in steps:
+            _sends(g, T, topo, core, steps[core], inc)
+        return
+    i, j = rank // GC, rank % GC
+
+    def load_w():
+        g.sync.dma_start(T.wb[:], T.w[:]).then_inc(T.sem.ldw, 16)
+
+    def load_x():
+        g.scalar.dma_start(T.xb[:], T.x[:]).then_inc(T.sem.ldx, 16)
+
+    def quant_w():
+        g.vector.wait_ge(T.sem.ldw, 16)
+        g.vector.quantize_mx(T.wq[:, j * WC:(j + 1) * WC], T.ws[:, j * WC:(j + 1) * WC], T.wb[:]).then_inc(T.sem.qw, 1)
+
+    def quant_x():
+        g.vector.wait_ge(T.sem.ldx, 16)
+        g.vector.quantize_mx(T.xo[:], T.xos[:], T.xb[:]).then_inc(T.sem.qx, 1)
+
+    for f in ((load_w, load_x, quant_w, quant_x) if ORDER[0][0] == "W" else (load_x, load_w, quant_x, quant_w)):
+        f()
+
+    _sends(g, T, topo, core, steps[core], inc)
+
+    seq = order[core]
+    for n, s in enumerate(seq):
+        if s == j:
+            g.tensor.wait_ge(T.sem.qw, 1)
+        else:
+            g.tensor.wait_ge(T.sem["sw%d" % s], inc[(core, "sw%d" % s)])
+        if i == j and s == j:
+            g.tensor.wait_ge(T.sem.qx, 1)
+            rhs, rsc = T.xo[:], T.xos[:]
+        else:
+            name = "sx%d" % s
+            if (core, name) not in inc:
+                name = "sx%d" % (s - s % 2)
+            g.tensor.wait_ge(T.sem[name], inc[(core, name)])
+            rhs, rsc = T.xq[:, s * XC:(s + 1) * XC], T.xs[:, s * XC:(s + 1) * XC]
+        mm = g.tensor.matmul_mx(T.acc[:, 0:XC], T.wq[:, s * WC:(s + 1) * WC], T.ws[:, s * WC:(s + 1) * WC], rhs, rsc,
+                                n == 0, n == len(seq) - 1)
+    mm.then_inc(T.sem.mm, 1)
+
+    g.vector.wait_ge(T.sem.mm, 1)
+    g.vector.tensor_copy(T.yb[:], T.acc[:, 0:XC]).then_inc(T.sem.cp, 1)
+    g.sync.wait_ge(T.sem.cp, 1)
+    g.sync.dma_start(T.y[:], T.yb[:]).then_inc(T.sem.st, 16)
+    g.sync.wait_ge(T.sem.st, 16)

@@ -3,29 +3,23 @@ from concourse.mybir import dt
 
 GR, GC = 4, 4
 XC, WC = 256, 128
+SL = XC + WC
 SIM_CORES = 512
-
-ORDER = ["Wh", "a", "Xh", "b", "f"]
-XH = "c"
-W_HELPERS = 1
-H_ENGINES = 8
-W_ON, X_ON = "low", "high"
-HELPER_DIE = "far"
 
 SCRATCH = {
     "wb": ("sbuf", [128, 4 * WC], "bfloat16"),
     "xb": ("sbuf", [128, 4 * XC], "bfloat16"),
-    "xo": ("sbuf", [128, XC], "float8_e4m3fn_x4"),
-    "xos": ("sbuf", [128, XC], "uint8"),
-    "xq": ("sbuf", [128, GC * XC], "float8_e4m3fn_x4"),
-    "xs": ("sbuf", [128, GC * XC], "uint8"),
-    "wq": ("sbuf", [128, GC * WC], "float8_e4m3fn_x4"),
-    "ws": ("sbuf", [128, GC * WC], "uint8"),
+    "oq": ("sbuf", [128, SL], "float8_e4m3fn_x4"),
+    "op": ("sbuf", [128, SL], "uint8"),
+    "tq": ("sbuf", [128, XC], "float8_e4m3fn_x4"),
+    "tp": ("sbuf", [128, XC], "uint8"),
+    "rq": ("sbuf", [128, GC * SL], "float8_e4m3fn_x4"),
+    "rp": ("sbuf", [128, GC * SL], "uint8"),
     "acc": ("psum", [128, 512], "float32"),
     "yb": ("sbuf", [128, XC], "float32"),
 }
-PLANE = {"xo": "xos", "xq": "xs", "wq": "ws"}
-SEMAPHORES = (["ldw", "ldx", "qw", "qx", "mm", "cp", "st", "sent", "sxo"]
+PLANE = {"oq": "op", "tq": "tp", "rq": "rp"}
+SEMAPHORES = (["ldw", "ldx", "qw", "qx", "mm", "cp", "st", "sent", "hw", "hx", "hc", "hd"]
               + ["sx%d" % s for s in range(GC)] + ["sw%d" % s for s in range(GC)])
 
 _CACHE = {}
@@ -35,31 +29,22 @@ def _bits(m):
     return bin(m).count("1")
 
 
-def _lowest(m, n):
-    out = 0
-    for e in range(m.bit_length()):
-        if m >> e & 1 and _bits(out) < n:
-            out |= 1 << e
-    return out
-
-
 def _plan(T, topo):
     if "p" in _CACHE:
         return _CACHE["p"]
     R = [[T.cores[i * GC + k] for k in range(GC)] for i in range(GR)]
-    steps, inc, order = {}, {}, {}
+    steps, inc, wsem, order = {}, {}, {}, {}
 
-    def add(src, waits, buf, lo, hi, dsts, sem, mask=None, engines=None):
+    def add(src, waits, buf, lo, hi, dsts, sem, mask=None, parts="cp"):
         m = mask
         if m is None:
             m = topo.mask(src, dsts[0][0])
             for d in dsts:
                 m &= topo.mask(src, d[0])
-        if engines:
-            m = _lowest(m, engines)
-        steps.setdefault(src, []).append({"wait": waits, "buf": buf, "lo": lo, "hi": hi, "dsts": dsts, "sem": sem, "mask": m})
+        steps.setdefault(src, []).append({"wait": waits, "buf": buf, "lo": lo, "hi": hi, "dsts": dsts, "sem": sem,
+                                          "mask": m, "parts": parts})
         for d in dsts:
-            inc[(d[0], sem)] = inc.get((d[0], sem), 0) + 2 * _bits(m)
+            inc[(d[0], sem)] = inc.get((d[0], sem), 0) + len(parts) * _bits(m)
 
     def hosts_of(c):
         others = [h for h in range(GR) if h != c]
@@ -68,58 +53,63 @@ def _plan(T, topo):
         cabl = [h for h in others if h not in (diag, mate)][0]
         return diag, mate, cabl
 
-    for i in range(GR):
-        diag, mate, cabl = hosts_of(i)
-        for j in range(GC):
-            me = R[i][j]
-            chipmates = [q for q in range(SIM_CORES) if q != me and topo.host(q) == topo.host(me) and topo.chip(q) == topo.chip(me)]
-            helpers = [q for q in chipmates if (topo.die(q) != topo.die(me)) == (HELPER_DIE == "far")]
-            off = topo.mask(me, R[i][(j + 1) % GC])
+    def helpers(i, j):
+        me = R[i][j]
+        chipmates = [q for q in range(SIM_CORES) if q != me and topo.host(q) == topo.host(me) and topo.chip(q) == topo.chip(me)]
+        far = [q for q in chipmates if topo.die(q) != topo.die(me)]
+        near = [q for q in chipmates if topo.die(q) == topo.die(me)]
+        return (far[1] if j % 2 == 0 else near[0]), far[0]
 
-            def on_chip(q, which):
-                m = topo.mask(me, q)
-                return {"low": m & off, "high": m & ~off, "all": m}[which]
+    for phase in range(4):
+        for i in range(GR):
+            diag, mate, cabl = hosts_of(i)
+            for j in range(GC):
+                me = R[i][j]
+                C, D = helpers(i, j)
+                off = topo.mask(me, R[i][(j + 1) % GC])
+                high = topo.mask(me, C) & topo.mask(me, D) & ~off
+                sx, sw = "sx%d" % j, "sw%d" % j
+                others = [k for k in range(GC) if k != j and k != i]
 
-            sw, sx = "sw%d" % j, "sx%d" % j
-            wdst = [(R[i][(j + t) % GC], "wq", j * WC) for t in range(1, GC)]
-            first, second = (cabl, mate) if j // 2 == i // 2 else (mate, cabl)
-            place = {"a": (R[first][i], "xq", j * XC), "b": (R[second][i], "xq", j * XC), "c": (R[i][i], "xq", j * XC)}
-            seen = set()
+                def wdst(k):
+                    return (R[i][k], "rq", j * SL + XC)
 
-            def need(name):
-                if name in seen:
-                    return []
-                seen.add(name)
-                return [name]
+                to_mate = (0, XC, (R[mate][i], "rq", j * SL), sx)
+                if j != i:
+                    to_own = (0, SL, (R[i][i], "rq", j * SL), sx)
+                    wsem[(R[i][i], j)] = sx
+                else:
+                    to_own = (XC, SL, wdst(others[2]), sw)
+                rank_job, d_job = (to_mate, to_own) if j % 2 == 0 else (to_own, to_mate)
 
-            for tok in ORDER:
-                if tok == "Wh":
-                    hs = helpers[:W_HELPERS]
-                    add(me, need("qw"), "wq", j * WC, (j + 1) * WC, [(h, "wq", j * WC) for h in hs], sw, on_chip(hs[0], W_ON))
-                    for n, h in enumerate(hs):
-                        add(h, [sw], "wq", j * WC, (j + 1) * WC, wdst[n::W_HELPERS], sw, None, H_ENGINES)
-                elif tok == "W":
-                    add(me, need("qw"), "wq", j * WC, (j + 1) * WC, wdst, sw)
-                elif tok in place:
-                    if place[tok][0] != me:
-                        add(me, need("qx"), "xo", 0, XC, [place[tok]], sx)
-                elif tok == "Xh":
-                    outs = [place[t] for t in XH if place[t][0] != me]
-                    if outs:
-                        h = helpers[W_HELPERS]
-                        add(me, need("qx"), "xo", 0, XC, [(h, "xo", 0)], "sxo", on_chip(h, X_ON))
-                        add(h, ["sxo"], "xo", 0, XC, outs, sx, None, H_ENGINES)
-                elif tok == "f" and j in (mate, cabl):
+                if phase == 0:
+                    add(me, ["qw"], "oq", XC, SL, [(C, "oq", XC), (D, "oq", XC)], "hw", high)
+                    add(C, ["hw"], "oq", XC, SL, [wdst(others[0])], sw)
+                    add(D, ["hw"], "oq", XC, SL, [wdst(others[1])], sw)
+                    if d_job[0] != 0:
+                        add(D, [], "oq", d_job[0], d_job[1], [d_job[2]], d_job[3])
+                elif phase == 1:
+                    Cf, Df = helpers(cabl, j)
+                    outs = [(R[cabl][i], "rq", j * SL), (R[diag][i], "rq", j * SL)]
+                    add(me, ["qx"], "oq", 0, XC, [(Df, "tq", 0)], "hd", None, "p")
+                    add(me, [], "oq", 0, XC, [(Cf, "tq", 0)], "hc", None, "c")
+                    add(Df, ["hd"], "tq", 0, XC, outs, sx, None, "p")
+                    add(Cf, ["hc"], "tq", 0, XC, outs, sx, None, "c")
+                elif phase == 2:
+                    if d_job[0] == 0:
+                        add(me, [], "oq", 0, XC, [(D, "oq", 0)], "hx", high)
+                        add(D, ["hx"], "oq", d_job[0], d_job[1], [d_job[2]], d_job[3])
+                else:
+                    add(me, [], "oq", rank_job[0], rank_job[1], [rank_job[2]], rank_job[3])
                     dj, mj, cj = hosts_of(j)
-                    p = j // 2 if i == cj else 1 - j // 2
-                    add(me, ["sx%d" % (2 * p), "sx%d" % (2 * p + 1)], "xq", 2 * p * XC, (2 * p + 2) * XC,
-                        [(R[dj][j], "xq", 2 * p * XC)], "sx%d" % (2 * p))
-                    order[me] = [2 * p, 2 * p + 1, 2 - 2 * p, 3 - 2 * p]
-            if j == i:
-                order[me] = [j] + [s for s in range(GC) if s != j]
-            elif j == diag:
-                order[me] = [0, 1, 2, 3]
-    _CACHE["p"] = (steps, inc, order)
+                    rest = [s for s in range(GC) if not (i == j and s == j)]
+                    if i == j:
+                        order[me] = [j] + [s for s in rest if s % 2 == 1] + [s for s in rest if s % 2 == 0]
+                    elif i == mj:
+                        order[me] = [s for s in rest if s % 2 == 0] + [s for s in rest if s % 2 == 1]
+                    else:
+                        order[me] = rest
+    _CACHE["p"] = (steps, inc, wsem, order)
     return _CACHE["p"]
 
 
@@ -129,8 +119,8 @@ def _sends(g, T, topo, core, steps, inc):
         for name in st["wait"]:
             g.wait_ge(T.sem[name], inc.get((core, name), 1))
         lo, hi, m = st["lo"], st["hi"], st["mask"]
-        for plane in (False, True):
-            if plane:
+        for part in st["parts"]:
+            if part == "p":
                 src = T[PLANE[st["buf"]]][:, lo:hi]
                 outs = [T[PLANE[b]][:, a:a + hi - lo] for (_, b, a) in st["dsts"]]
             else:
@@ -150,7 +140,7 @@ def _sends(g, T, topo, core, steps, inc):
 
 
 def rank_program(g, core, T, topo):
-    steps, inc, order = _plan(T, topo)
+    steps, inc, wsem, order = _plan(T, topo)
     rank = T.rank_of(core)
     if rank is None:
         if core in steps:
@@ -158,22 +148,12 @@ def rank_program(g, core, T, topo):
         return
     i, j = rank // GC, rank % GC
 
-    def load_w():
-        g.sync.dma_start(T.wb[:], T.w[:]).then_inc(T.sem.ldw, 16)
-
-    def load_x():
-        g.scalar.dma_start(T.xb[:], T.x[:]).then_inc(T.sem.ldx, 16)
-
-    def quant_w():
-        g.vector.wait_ge(T.sem.ldw, 16)
-        g.vector.quantize_mx(T.wq[:, j * WC:(j + 1) * WC], T.ws[:, j * WC:(j + 1) * WC], T.wb[:]).then_inc(T.sem.qw, 1)
-
-    def quant_x():
-        g.vector.wait_ge(T.sem.ldx, 16)
-        g.vector.quantize_mx(T.xo[:], T.xos[:], T.xb[:]).then_inc(T.sem.qx, 1)
-
-    for f in ((load_w, load_x, quant_w, quant_x) if ORDER[0][0] == "W" else (load_x, load_w, quant_x, quant_w)):
-        f()
+    g.sync.dma_start(T.wb[:], T.w[:]).then_inc(T.sem.ldw, 16)
+    g.scalar.dma_start(T.xb[:], T.x[:]).then_inc(T.sem.ldx, 16)
+    g.vector.wait_ge(T.sem.ldw, 16)
+    g.vector.quantize_mx(T.oq[:, XC:SL], T.op[:, XC:SL], T.wb[:]).then_inc(T.sem.qw, 1)
+    g.vector.wait_ge(T.sem.ldx, 16)
+    g.vector.quantize_mx(T.oq[:, 0:XC], T.op[:, 0:XC], T.xb[:]).then_inc(T.sem.qx, 1)
 
     _sends(g, T, topo, core, steps[core], inc)
 
@@ -181,19 +161,19 @@ def rank_program(g, core, T, topo):
     for n, s in enumerate(seq):
         if s == j:
             g.tensor.wait_ge(T.sem.qw, 1)
+            lhs, lsc = T.oq[:, XC:SL], T.op[:, XC:SL]
         else:
-            g.tensor.wait_ge(T.sem["sw%d" % s], inc[(core, "sw%d" % s)])
+            name = wsem.get((core, s), "sw%d" % s)
+            g.tensor.wait_ge(T.sem[name], inc[(core, name)])
+            lhs, lsc = T.rq[:, s * SL + XC:(s + 1) * SL], T.rp[:, s * SL + XC:(s + 1) * SL]
         if i == j and s == j:
             g.tensor.wait_ge(T.sem.qx, 1)
-            rhs, rsc = T.xo[:], T.xos[:]
+            rhs, rsc = T.oq[:, 0:XC], T.op[:, 0:XC]
         else:
             name = "sx%d" % s
-            if (core, name) not in inc:
-                name = "sx%d" % (s - s % 2)
             g.tensor.wait_ge(T.sem[name], inc[(core, name)])
-            rhs, rsc = T.xq[:, s * XC:(s + 1) * XC], T.xs[:, s * XC:(s + 1) * XC]
-        mm = g.tensor.matmul_mx(T.acc[:, 0:XC], T.wq[:, s * WC:(s + 1) * WC], T.ws[:, s * WC:(s + 1) * WC], rhs, rsc,
-                                n == 0, n == len(seq) - 1)
+            rhs, rsc = T.rq[:, s * SL:s * SL + XC], T.rp[:, s * SL:s * SL + XC]
+        mm = g.tensor.matmul_mx(T.acc[:, 0:XC], lhs, lsc, rhs, rsc, n == 0, n == len(seq) - 1)
     mm.then_inc(T.sem.mm, 1)
 
     g.vector.wait_ge(T.sem.mm, 1)

@@ -58,16 +58,16 @@ def _plan(T, topo):
         chipmates = [q for q in range(SIM_CORES) if q != me and topo.host(q) == topo.host(me) and topo.chip(q) == topo.chip(me)]
         far = [q for q in chipmates if topo.die(q) != topo.die(me)]
         near = [q for q in chipmates if topo.die(q) == topo.die(me)]
-        return (far[1] if j % 2 == 0 else near[0]), far[0]
+        return ((near[0], far[1]) if j % 2 == 0 else (far[1], near[0])) + (far[0],)
 
     for phase in range(4):
         for i in range(GR):
             diag, mate, cabl = hosts_of(i)
             for j in range(GC):
                 me = R[i][j]
-                C, D = helpers(i, j)
+                C, D, E = helpers(i, j)
                 off = topo.mask(me, R[i][(j + 1) % GC])
-                high = topo.mask(me, C) & topo.mask(me, D) & ~off
+                high = topo.mask(me, C) & topo.mask(me, D) & topo.mask(me, E) & ~off
                 sx, sw = "sx%d" % j, "sw%d" % j
                 others = [k for k in range(GC) if k != j and k != i]
 
@@ -80,35 +80,42 @@ def _plan(T, topo):
                     wsem[(R[i][i], j)] = sx
                 else:
                     to_own = (XC, SL, wdst(others[2]), sw)
-                rank_job, d_job = (to_mate, to_own) if j % 2 == 0 else (to_own, to_mate)
+                rank_job, e_job = (to_mate, to_own) if j % 2 == 0 else (to_own, to_mate)
 
                 if phase == 0:
-                    add(me, ["qw"], "oq", XC, SL, [(C, "oq", XC), (D, "oq", XC)], "hw", high)
+                    add(me, ["qw"], "oq", XC, SL, [(C, "oq", XC), (E, "oq", XC)], "hw", high, "c")
+                    add(me, [], "oq", XC, SL, [(C, "oq", XC), (D, "oq", XC), (E, "oq", XC)], "hw", high, "p")
                     add(C, ["hw"], "oq", XC, SL, [wdst(others[0])], sw)
-                    add(D, ["hw"], "oq", XC, SL, [wdst(others[1])], sw)
-                    if d_job[0] != 0:
-                        add(D, [], "oq", d_job[0], d_job[1], [d_job[2]], d_job[3])
+                    add(E, ["hw"], "oq", XC, SL, [wdst(others[1])], sw, None, "c")
+                    add(D, ["hw"], "oq", XC, SL, [wdst(others[1])], sw, None, "p")
+                    if e_job[0] != 0:
+                        add(E, [], "oq", e_job[0], e_job[1], [e_job[2]], e_job[3])
                 elif phase == 1:
-                    Cf, Df = helpers(cabl, j)
+                    Cf, Df, Ef = helpers(cabl, j)
                     outs = [(R[cabl][i], "rq", j * SL), (R[diag][i], "rq", j * SL)]
-                    add(me, ["qx"], "oq", 0, XC, [(Df, "tq", 0)], "hd", None, "p")
-                    add(me, [], "oq", 0, XC, [(Cf, "tq", 0)], "hc", None, "c")
-                    add(Df, ["hd"], "tq", 0, XC, outs, sx, None, "p")
-                    add(Cf, ["hc"], "tq", 0, XC, outs, sx, None, "c")
+                    if j % 2 == 1:
+                        outs.reverse()
+                    add(me, ["qx"], "oq", 0, XC, [(Cf, "tq", 0)], "hc", None, "c")
+                    add(me, [], "oq", 0, XC, [(Df, "tq", 0)], "hd", None, "p")
+                    for h, name, part in ((Cf, "hc", "c"), (Df, "hd", "p")):
+                        m = topo.mask(h, outs[0][0]) & topo.mask(h, outs[1][0])
+                        add(h, [name], "tq", 0, XC, outs[0:1], sx, m, part)
+                        add(h, [], "tq", 0, XC, outs[1:2], sx, m, part)
                 elif phase == 2:
-                    if d_job[0] == 0:
-                        add(me, [], "oq", 0, XC, [(D, "oq", 0)], "hx", high)
-                        add(D, ["hx"], "oq", d_job[0], d_job[1], [d_job[2]], d_job[3])
+                    if e_job[0] == 0:
+                        add(me, [], "oq", 0, XC, [(E, "oq", 0)], "hx", high)
+                        add(E, ["hx"], "oq", e_job[0], e_job[1], [e_job[2]], e_job[3])
                 else:
                     add(me, [], "oq", rank_job[0], rank_job[1], [rank_job[2]], rank_job[3])
                     dj, mj, cj = hosts_of(j)
                     rest = [s for s in range(GC) if not (i == j and s == j)]
+                    even, odd = [s for s in rest if s % 2 == 0], [s for s in rest if s % 2 == 1]
                     if i == j:
-                        order[me] = [j] + [s for s in rest if s % 2 == 1] + [s for s in rest if s % 2 == 0]
-                    elif i == mj:
-                        order[me] = [s for s in rest if s % 2 == 0] + [s for s in rest if s % 2 == 1]
+                        order[me] = [j] + odd + even
+                    elif i == mj or i == cj:
+                        order[me] = even + odd
                     else:
-                        order[me] = rest
+                        order[me] = odd + even
     _CACHE["p"] = (steps, inc, wsem, order)
     return _CACHE["p"]
 

@@ -3,6 +3,7 @@ from concourse.mybir import dt
 
 GR, GC = 4, 4
 XC, WC = 256, 128
+HC = XC // 2
 SL = XC + WC
 SIM_CORES = 512
 
@@ -19,7 +20,7 @@ SCRATCH = {
     "yb": ("sbuf", [128, XC], "float32"),
 }
 PLANE = {"oq": "op", "tq": "tp", "rq": "rp"}
-SEMAPHORES = (["ldw", "ldx", "qw", "qx", "mm", "cp", "st", "sent", "hw", "hx", "hc", "hd"]
+SEMAPHORES = (["ldw", "ldx", "qw", "qx", "mm", "cp", "st", "sent", "hw", "hx", "hp", "hc", "hd"]
               + ["sx%d" % s for s in range(GC)] + ["sw%d" % s for s in range(GC)])
 
 _CACHE = {}
@@ -33,18 +34,26 @@ def _plan(T, topo):
     if "p" in _CACHE:
         return _CACHE["p"]
     R = [[T.cores[i * GC + k] for k in range(GC)] for i in range(GR)]
-    steps, inc, wsem, order = {}, {}, {}, {}
+    steps, inc, order = {}, {}, {}
 
-    def add(src, waits, buf, lo, hi, dsts, sem, mask=None, parts="cp"):
+    def call(src, waits, transfers):
+        steps.setdefault(src, []).append({"wait": waits, "tr": transfers})
+        for (part, buf, lo, hi, dsts, sem, m) in transfers:
+            for d in dsts:
+                inc[(d[0], sem)] = inc.get((d[0], sem), 0) + _bits(m)
+
+    def add(src, waits, buf, lo, hi, dsts, sem, mask, part):
         m = mask
         if m is None:
             m = topo.mask(src, dsts[0][0])
             for d in dsts:
                 m &= topo.mask(src, d[0])
-        steps.setdefault(src, []).append({"wait": waits, "buf": buf, "lo": lo, "hi": hi, "dsts": dsts, "sem": sem,
-                                          "mask": m, "parts": parts})
-        for d in dsts:
-            inc[(d[0], sem)] = inc.get((d[0], sem), 0) + len(parts) * _bits(m)
+        call(src, waits, [(part, buf, lo, hi, dsts, sem, m)])
+
+    def cut(m, n, k):
+        e = [b for b in range(m.bit_length()) if m >> b & 1]
+        w = len(e) // n
+        return sum(1 << b for b in e[k * w:(k + 1) * w])
 
     def hosts_of(c):
         others = [h for h in range(GR) if h != c]
@@ -58,55 +67,65 @@ def _plan(T, topo):
         chipmates = [q for q in range(SIM_CORES) if q != me and topo.host(q) == topo.host(me) and topo.chip(q) == topo.chip(me)]
         far = [q for q in chipmates if topo.die(q) != topo.die(me)]
         near = [q for q in chipmates if topo.die(q) == topo.die(me)]
-        return ((near[0], far[1]) if j % 2 == 0 else (far[1], near[0])) + (far[0],)
+        if j % 2 == 0:
+            return far[0], near[0], far[1], far[2], far[3]
+        return near[0], far[0], near[1], far[1], far[2]
 
-    for phase in range(4):
+    for phase in range(3):
         for i in range(GR):
             diag, mate, cabl = hosts_of(i)
             for j in range(GC):
                 me = R[i][j]
-                C, D, E = helpers(i, j)
+                C1, C2, D, E1, E2 = helpers(i, j)
                 off = topo.mask(me, R[i][(j + 1) % GC])
-                high = topo.mask(me, C) & topo.mask(me, D) & topo.mask(me, E) & ~off
+                high = ~off
+                for h in (C1, C2, D, E1, E2):
+                    high &= topo.mask(me, h)
                 sx, sw = "sx%d" % j, "sw%d" % j
-                others = [k for k in range(GC) if k != j and k != i]
+                ks = [k for k in range(GC) if k != j]
 
                 def wdst(k):
                     return (R[i][k], "rq", j * SL + XC)
 
-                to_mate = (0, XC, (R[mate][i], "rq", j * SL), sx)
-                if j != i:
-                    to_own = (0, SL, (R[i][i], "rq", j * SL), sx)
-                    wsem[(R[i][i], j)] = sx
-                else:
-                    to_own = (XC, SL, wdst(others[2]), sw)
-                rank_job, e_job = (to_mate, to_own) if j % 2 == 0 else (to_own, to_mate)
+                near = [R[mate][i]] + ([R[i][i]] if j != i else [])
+                if j % 2 == 1:
+                    near.reverse()
+                r_dst, e_dst = near[0], (near[1] if len(near) > 1 else None)
 
                 if phase == 0:
-                    add(me, ["qw"], "oq", XC, SL, [(C, "oq", XC), (E, "oq", XC)], "hw", high, "c")
-                    add(me, [], "oq", XC, SL, [(C, "oq", XC), (D, "oq", XC), (E, "oq", XC)], "hw", high, "p")
-                    add(C, ["hw"], "oq", XC, SL, [wdst(others[0])], sw)
-                    add(E, ["hw"], "oq", XC, SL, [wdst(others[1])], sw, None, "c")
-                    add(D, ["hw"], "oq", XC, SL, [wdst(others[1])], sw, None, "p")
-                    if e_job[0] != 0:
-                        add(E, [], "oq", e_job[0], e_job[1], [e_job[2]], e_job[3])
+                    add(me, ["qw"], "oq", XC, SL, [(C1, "oq", XC), (C2, "oq", XC), (E2, "oq", XC)], "hw", high, "c")
+                    add(me, [], "oq", XC, SL, [(D, "oq", XC), (E1, "oq", XC)], "hw", high, "p")
+                    add(C1, ["hw"], "oq", XC, SL, [wdst(ks[0])], sw, None, "c")
+                    add(C2, ["hw"], "oq", XC, SL, [wdst(ks[1])], sw, None, "c")
+                    add(E2, ["hw"], "oq", XC, SL, [wdst(ks[2])], sw, None, "c")
+                    add(D, ["hw"], "oq", XC, SL, [wdst(ks[0])], sw, None, "p")
+                    add(D, [], "oq", XC, SL, [wdst(ks[1])], sw, None, "p")
+                    add(E1, ["hw"], "oq", XC, SL, [wdst(ks[2])], sw, None, "p")
                 elif phase == 1:
-                    Cf, Df, Ef = helpers(cabl, j)
-                    outs = [(R[cabl][i], "rq", j * SL), (R[diag][i], "rq", j * SL)]
+                    C1f, C2f, Df, E1f, E2f = helpers(cabl, j)
+                    outs = [R[cabl][i], R[diag][i]]
                     if j % 2 == 1:
                         outs.reverse()
-                    add(me, ["qx"], "oq", 0, XC, [(Cf, "tq", 0)], "hc", None, "c")
-                    add(me, [], "oq", 0, XC, [(Df, "tq", 0)], "hd", None, "p")
-                    for h, name, part in ((Cf, "hc", "c"), (Df, "hd", "p")):
-                        m = topo.mask(h, outs[0][0]) & topo.mask(h, outs[1][0])
-                        add(h, [name], "tq", 0, XC, outs[0:1], sx, m, part)
-                        add(h, [], "tq", 0, XC, outs[1:2], sx, m, part)
-                elif phase == 2:
-                    if e_job[0] == 0:
-                        add(me, [], "oq", 0, XC, [(E, "oq", 0)], "hx", high)
-                        add(E, ["hx"], "oq", e_job[0], e_job[1], [e_job[2]], e_job[3])
+                    halves = [("c", "oq", 0, HC, [(C1f, "tq", 0)], "hc", cut(off, 2, 0)),
+                              ("c", "oq", HC, XC, [(C2f, "tq", HC)], "hc", cut(off, 2, 1))]
+                    planes = [("p", "oq", 0, XC, [(Df, "tq", 0)], "hd", cut(off, 2, 0)),
+                              ("p", "oq", 0, XC, [(r_dst, "rq", j * SL)], sx, cut(off, 2, 1))]
+                    if e_dst is not None:
+                        halves += [("c", "oq", 0, HC, [(E1, "oq", 0)], "hx", cut(high, 2, 0)),
+                                   ("c", "oq", HC, XC, [(E2, "oq", HC)], "hx", cut(high, 2, 1))]
+                        planes += [("p", "oq", 0, XC, [(E1, "oq", 0)], "hp", high)]
+                    call(me, ["qx"], halves)
+                    call(me, [], planes)
+                    for h, lo, hi, name, part in ((C1f, 0, HC, "hc", "c"), (C2f, HC, XC, "hc", "c"), (Df, 0, XC, "hd", "p")):
+                        m = topo.mask(h, outs[0]) & topo.mask(h, outs[1])
+                        add(h, [name], "tq", lo, hi, [(outs[0], "rq", j * SL + lo)], sx, m, part)
+                        add(h, [], "tq", lo, hi, [(outs[1], "rq", j * SL + lo)], sx, m, part)
+                    if e_dst is not None:
+                        add(E1, ["hx"], "oq", 0, HC, [(e_dst, "rq", j * SL)], sx, None, "c")
+                        add(E2, ["hx"], "oq", HC, XC, [(e_dst, "rq", j * SL + HC)], sx, None, "c")
+                        add(E1, ["hp"], "oq", 0, XC, [(e_dst, "rq", j * SL)], sx, None, "p")
                 else:
-                    add(me, [], "oq", rank_job[0], rank_job[1], [rank_job[2]], rank_job[3])
+                    add(me, [], "oq", 0, XC, [(r_dst, "rq", j * SL)], sx, None, "c")
                     dj, mj, cj = hosts_of(j)
                     rest = [s for s in range(GC) if not (i == j and s == j)]
                     even, odd = [s for s in rest if s % 2 == 0], [s for s in rest if s % 2 == 1]
@@ -116,7 +135,7 @@ def _plan(T, topo):
                         order[me] = even + odd
                     else:
                         order[me] = odd + even
-    _CACHE["p"] = (steps, inc, wsem, order)
+    _CACHE["p"] = (steps, inc, order)
     return _CACHE["p"]
 
 
@@ -125,29 +144,31 @@ def _sends(g, T, topo, core, steps, inc):
     for st in steps:
         for name in st["wait"]:
             g.wait_ge(T.sem[name], inc.get((core, name), 1))
-        lo, hi, m = st["lo"], st["hi"], st["mask"]
-        for part in st["parts"]:
+        trs = []
+        for (part, buf, lo, hi, dsts, sem, m) in st["tr"]:
             if part == "p":
-                src = T[PLANE[st["buf"]]][:, lo:hi]
-                outs = [T[PLANE[b]][:, a:a + hi - lo] for (_, b, a) in st["dsts"]]
+                src = T[PLANE[buf]][:, lo:hi]
+                outs = [T[PLANE[b]][:, a:a + hi - lo] for (_, b, a) in dsts]
             else:
-                src = T[st["buf"]][:, lo:hi].bitcast(dt.uint8)
-                outs = [T[b][:, a:a + hi - lo].bitcast(dt.uint8) for (_, b, a) in st["dsts"]]
-            ids = [topo.addr(d[0], core) for d in st["dsts"]]
-            if len(outs) == 1:
-                g.remote_dma(out_ap=outs[0], in_ap=src, remote_sem=T.sem[st["sem"]], local_sem=T.sem.sent,
-                             pid=ids[0][1], routing_id=ids[0][0], dma_engine_mask=m)
-            else:
-                g.remote_dma_fused([RemoteDMATransfer(dst_ids=[DstId(rid=a, pnc=b) for (a, b) in ids], dma_engine_mask=m,
-                                                      remote_sem=T.sem[st["sem"]], srcs=[src], dsts=outs)],
-                                   local_sem=T.sem.sent)
+                src = T[buf][:, lo:hi].bitcast(dt.uint8)
+                outs = [T[b][:, a:a + hi - lo].bitcast(dt.uint8) for (_, b, a) in dsts]
+            ids = [topo.addr(d[0], core) for d in dsts]
+            trs.append((src, outs, ids, sem, m))
             sent += _bits(m)
+        if len(trs) == 1 and len(trs[0][1]) == 1:
+            src, outs, ids, sem, m = trs[0]
+            g.remote_dma(out_ap=outs[0], in_ap=src, remote_sem=T.sem[sem], local_sem=T.sem.sent,
+                         pid=ids[0][1], routing_id=ids[0][0], dma_engine_mask=m)
+        else:
+            g.remote_dma_fused([RemoteDMATransfer(dst_ids=[DstId(rid=a, pnc=b) for (a, b) in ids], dma_engine_mask=m,
+                                                  remote_sem=T.sem[sem], srcs=[src], dsts=outs)
+                                for (src, outs, ids, sem, m) in trs], local_sem=T.sem.sent)
     if sent:
         g.wait_ge(T.sem.sent, sent)
 
 
 def rank_program(g, core, T, topo):
-    steps, inc, wsem, order = _plan(T, topo)
+    steps, inc, order = _plan(T, topo)
     rank = T.rank_of(core)
     if rank is None:
         if core in steps:
@@ -170,7 +191,7 @@ def rank_program(g, core, T, topo):
             g.tensor.wait_ge(T.sem.qw, 1)
             lhs, lsc = T.oq[:, XC:SL], T.op[:, XC:SL]
         else:
-            name = wsem.get((core, s), "sw%d" % s)
+            name = "sw%d" % s
             g.tensor.wait_ge(T.sem[name], inc[(core, name)])
             lhs, lsc = T.rq[:, s * SL + XC:(s + 1) * SL], T.rp[:, s * SL + XC:(s + 1) * SL]
         if i == j and s == j:

from concourse.bass import DstId, RemoteDMATransfer
from concourse.mybir import dt

GR, GC = 4, 4
XC, WC = 256, 128
HC = XC // 2
SL = XC + WC
SIM_CORES = 512

SCRATCH = {
    "wb": ("sbuf", [128, 4 * WC], "bfloat16"),
    "xb": ("sbuf", [128, 4 * XC], "bfloat16"),
    "oq": ("sbuf", [128, SL], "float8_e4m3fn_x4"),
    "op": ("sbuf", [128, SL], "uint8"),
    "tq": ("sbuf", [128, XC], "float8_e4m3fn_x4"),
    "tp": ("sbuf", [128, XC], "uint8"),
    "rq": ("sbuf", [128, GC * SL], "float8_e4m3fn_x4"),
    "rp": ("sbuf", [128, GC * SL], "uint8"),
    "acc": ("psum", [128, 512], "float32"),
    "yb": ("sbuf", [128, XC], "float32"),
}
PLANE = {"oq": "op", "tq": "tp", "rq": "rp"}
SEMAPHORES = (["ldw", "ldx", "qw", "qx", "mm", "cp", "st", "sent", "hw", "hx", "hp", "hc", "hd"]
              + ["sx%d" % s for s in range(GC)] + ["sw%d" % s for s in range(GC)])

_CACHE = {}


def _bits(m):
    return bin(m).count("1")


def _plan(T, topo):
    if "p" in _CACHE:
        return _CACHE["p"]
    R = [[T.cores[i * GC + k] for k in range(GC)] for i in range(GR)]
    steps, inc, order = {}, {}, {}

    def call(src, waits, transfers):
        steps.setdefault(src, []).append({"wait": waits, "tr": transfers})
        for (part, buf, lo, hi, dsts, sem, m) in transfers:
            for d in dsts:
                inc[(d[0], sem)] = inc.get((d[0], sem), 0) + _bits(m)

    def add(src, waits, buf, lo, hi, dsts, sem, mask, part):
        m = mask
        if m is None:
            m = topo.mask(src, dsts[0][0])
            for d in dsts:
                m &= topo.mask(src, d[0])
        call(src, waits, [(part, buf, lo, hi, dsts, sem, m)])

    def cut(m, n, k):
        e = [b for b in range(m.bit_length()) if m >> b & 1]
        w = len(e) // n
        return sum(1 << b for b in e[k * w:(k + 1) * w])

    def hosts_of(c):
        others = [h for h in range(GR) if h != c]
        diag = [h for h in others if not topo.may_write(R[c][0], R[h][0])][0]
        mate = [h for h in others if h != diag and topo.rack(topo.host(R[h][0])) == topo.rack(topo.host(R[c][0]))][0]
        cabl = [h for h in others if h not in (diag, mate)][0]
        return diag, mate, cabl

    def helpers(i, j):
        me = R[i][j]
        chipmates = [q for q in range(SIM_CORES) if q != me and topo.host(q) == topo.host(me) and topo.chip(q) == topo.chip(me)]
        far = [q for q in chipmates if topo.die(q) != topo.die(me)]
        near = [q for q in chipmates if topo.die(q) == topo.die(me)]
        if j % 2 == 0:
            return far[0], near[0], far[1], far[2], far[3]
        return near[0], far[0], near[1], far[1], far[2]

    for phase in range(3):
        for i in range(GR):
            diag, mate, cabl = hosts_of(i)
            for j in range(GC):
                me = R[i][j]
                C1, C2, D, E1, E2 = helpers(i, j)
                off = topo.mask(me, R[i][(j + 1) % GC])
                high = ~off
                for h in (C1, C2, D, E1, E2):
                    high &= topo.mask(me, h)
                sx, sw = "sx%d" % j, "sw%d" % j
                ks = [k for k in range(GC) if k != j]

                def wdst(k):
                    return (R[i][k], "rq", j * SL + XC)

                near = [R[mate][i]] + ([R[i][i]] if j != i else [])
                if j % 2 == 1:
                    near.reverse()
                r_dst, e_dst = near[0], (near[1] if len(near) > 1 else None)

                if phase == 0:
                    add(me, ["qw"], "oq", XC, SL, [(C1, "oq", XC), (C2, "oq", XC), (E2, "oq", XC)], "hw", high, "c")
                    add(me, [], "oq", XC, SL, [(D, "oq", XC), (E1, "oq", XC)], "hw", high, "p")
                    add(C1, ["hw"], "oq", XC, SL, [wdst(ks[0])], sw, None, "c")
                    add(C2, ["hw"], "oq", XC, SL, [wdst(ks[1])], sw, None, "c")
                    add(E2, ["hw"], "oq", XC, SL, [wdst(ks[2])], sw, None, "c")
                    add(D, ["hw"], "oq", XC, SL, [wdst(ks[0])], sw, None, "p")
                    add(D, [], "oq", XC, SL, [wdst(ks[1])], sw, None, "p")
                    add(E1, ["hw"], "oq", XC, SL, [wdst(ks[2])], sw, None, "p")
                elif phase == 1:
                    C1f, C2f, Df, E1f, E2f = helpers(cabl, j)
                    outs = [R[cabl][i], R[diag][i]]
                    if j % 2 == 1:
                        outs.reverse()
                    halves = [("c", "oq", 0, HC, [(C1f, "tq", 0)], "hc", cut(off, 2, 0)),
                              ("c", "oq", HC, XC, [(C2f, "tq", HC)], "hc", cut(off, 2, 1))]
                    planes = [("p", "oq", 0, XC, [(Df, "tq", 0)], "hd", cut(off, 2, 0)),
                              ("p", "oq", 0, XC, [(r_dst, "rq", j * SL)], sx, cut(off, 2, 1))]
                    if e_dst is not None:
                        halves += [("c", "oq", 0, HC, [(E1, "oq", 0)], "hx", cut(high, 2, 0)),
                                   ("c", "oq", HC, XC, [(E2, "oq", HC)], "hx", cut(high, 2, 1))]
                        planes += [("p", "oq", 0, XC, [(E1, "oq", 0)], "hp", high)]
                    call(me, ["qx"], halves)
                    call(me, [], planes)
                    for h, lo, hi, name, part in ((C1f, 0, HC, "hc", "c"), (C2f, HC, XC, "hc", "c"), (Df, 0, XC, "hd", "p")):
                        m = topo.mask(h, outs[0]) & topo.mask(h, outs[1])
                        add(h, [name], "tq", lo, hi, [(outs[0], "rq", j * SL + lo)], sx, m, part)
                        add(h, [], "tq", lo, hi, [(outs[1], "rq", j * SL + lo)], sx, m, part)
                    if e_dst is not None:
                        add(E1, ["hx"], "oq", 0, HC, [(e_dst, "rq", j * SL)], sx, None, "c")
                        add(E2, ["hx"], "oq", HC, XC, [(e_dst, "rq", j * SL + HC)], sx, None, "c")
                        add(E1, ["hp"], "oq", 0, XC, [(e_dst, "rq", j * SL)], sx, None, "p")
                else:
                    add(me, [], "oq", 0, XC, [(r_dst, "rq", j * SL)], sx, None, "c")
                    dj, mj, cj = hosts_of(j)
                    rest = [s for s in range(GC) if not (i == j and s == j)]
                    even, odd = [s for s in rest if s % 2 == 0], [s for s in rest if s % 2 == 1]
                    if i == j:
                        order[me] = [j] + odd + even
                    elif i == mj or i == cj:
                        order[me] = even + odd
                    else:
                        order[me] = odd + even
    _CACHE["p"] = (steps, inc, order)
    return _CACHE["p"]


def _sends(g, T, topo, core, steps, inc):
    sent = 0
    for st in steps:
        for name in st["wait"]:
            g.wait_ge(T.sem[name], inc.get((core, name), 1))
        trs = []
        for (part, buf, lo, hi, dsts, sem, m) in st["tr"]:
            if part == "p":
                src = T[PLANE[buf]][:, lo:hi]
                outs = [T[PLANE[b]][:, a:a + hi - lo] for (_, b, a) in dsts]
            else:
                src = T[buf][:, lo:hi].bitcast(dt.uint8)
                outs = [T[b][:, a:a + hi - lo].bitcast(dt.uint8) for (_, b, a) in dsts]
            ids = [topo.addr(d[0], core) for d in dsts]
            trs.append((src, outs, ids, sem, m))
            sent += _bits(m)
        if len(trs) == 1 and len(trs[0][1]) == 1:
            src, outs, ids, sem, m = trs[0]
            g.remote_dma(out_ap=outs[0], in_ap=src, remote_sem=T.sem[sem], local_sem=T.sem.sent,
                         pid=ids[0][1], routing_id=ids[0][0], dma_engine_mask=m)
        else:
            g.remote_dma_fused([RemoteDMATransfer(dst_ids=[DstId(rid=a, pnc=b) for (a, b) in ids], dma_engine_mask=m,
                                                  remote_sem=T.sem[sem], srcs=[src], dsts=outs)
                                for (src, outs, ids, sem, m) in trs], local_sem=T.sem.sent)
    if sent:
        g.wait_ge(T.sem.sent, sent)


def rank_program(g, core, T, topo):
    steps, inc, order = _plan(T, topo)
    rank = T.rank_of(core)
    if rank is None:
        if core in steps:
            _sends(g, T, topo, core, steps[core], inc)
        return
    i, j = rank // GC, rank % GC

    g.sync.dma_start(T.wb[:], T.w[:]).then_inc(T.sem.ldw, 16)
    g.scalar.dma_start(T.xb[:], T.x[:]).then_inc(T.sem.ldx, 16)
    g.vector.wait_ge(T.sem.ldw, 16)
    g.vector.quantize_mx(T.oq[:, XC:SL], T.op[:, XC:SL], T.wb[:]).then_inc(T.sem.qw, 1)
    g.vector.wait_ge(T.sem.ldx, 16)
    g.vector.quantize_mx(T.oq[:, 0:XC], T.op[:, 0:XC], T.xb[:]).then_inc(T.sem.qx, 1)

    _sends(g, T, topo, core, steps[core], inc)

    seq = order[core]
    for n, s in enumerate(seq):
        if s == j:
            g.tensor.wait_ge(T.sem.qw, 1)
            lhs, lsc = T.oq[:, XC:SL], T.op[:, XC:SL]
        else:
            name = "sw%d" % s
            g.tensor.wait_ge(T.sem[name], inc[(core, name)])
            lhs, lsc = T.rq[:, s * SL + XC:(s + 1) * SL], T.rp[:, s * SL + XC:(s + 1) * SL]
        if i == j and s == j:
            g.tensor.wait_ge(T.sem.qx, 1)
            rhs, rsc = T.oq[:, 0:XC], T.op[:, 0:XC]
        else:
            name = "sx%d" % s
            g.tensor.wait_ge(T.sem[name], inc[(core, name)])
            rhs, rsc = T.rq[:, s * SL:s * SL + XC], T.rp[:, s * SL:s * SL + XC]
        mm = g.tensor.matmul_mx(T.acc[:, 0:XC], lhs, lsc, rhs, rsc, n == 0, n == len(seq) - 1)
    mm.then_inc(T.sem.mm, 1)

    g.vector.wait_ge(T.sem.mm, 1)
    g.vector.tensor_copy(T.yb[:], T.acc[:, 0:XC]).then_inc(T.sem.cp, 1)
    g.sync.wait_ge(T.sem.cp, 1)
    g.sync.dma_start(T.y[:], T.yb[:]).then_inc(T.sem.st, 16)
    g.sync.wait_ge(T.sem.st, 16)
